import numpy as np
import ml_dtypes


def mxq(x, axis, fmt="e4m3"):
    dtype, down = {"e4m3": (ml_dtypes.float8_e4m3fn, 7), "e5m2": (ml_dtypes.float8_e5m2, 14)}[fmt]
    v = np.moveaxis(np.asarray(x, np.float32).astype(ml_dtypes.bfloat16).astype(np.float64), axis, -1)
    blocks = v.reshape(v.shape[:-1] + (-1, 32))
    amax = np.abs(blocks).max(-1, keepdims=True)
    byte = np.maximum(np.where(amax > 0, np.frexp(amax)[1] - 1 + 127, 0) - down, 1)
    scale = np.exp2(byte - 127.0)
    codes = (blocks / scale).astype(np.float32).astype(dtype).astype(np.float64)
    return np.moveaxis((codes * scale).reshape(v.shape), -1, axis)


WIDE = False


def mx_kscale(k):
    if not WIDE:
        return np.ones(k)
    levels = np.array([10, -10, 5, -5, 0])
    if k % 512:
        return np.exp2(np.random.permutation(np.resize(levels, k // 32))).repeat(32)
    a = np.empty((k // 512, 16))
    for p in range(k // 512):
        a[p, :8] = np.random.permutation(np.resize(levels, 8))
        for g in range(8):
            far = levels[np.abs(levels - a[p, g]) >= 10]
            a[p, g + 8] = far[np.random.randint(len(far))]
    return np.exp2(a.ravel()).repeat(32)


BF16 = ml_dtypes.bfloat16


def bf(x):
    return np.asarray(x, np.float32).astype(BF16)


def f64(x):
    return np.asarray(x).astype(np.float64)


E2M1 = np.array([0.0, 0.5, 1.0, 1.5, 2.0, 3.0, 4.0, 6.0, -0.0, -0.5, -1.0, -1.5, -2.0, -3.0, -4.0, -6.0])


def pack_weight(w, fmt):
    k, n = w.shape
    w = f64(bf(w)).reshape(k // 32, 32, n)
    amax = np.abs(w).max(1)
    if fmt == "e4m3":
        byte = np.frexp(amax)[1] - 1 + 127 - 7
    else:
        mant, ex = np.frexp(amax / 6.0)
        byte = np.where(mant > 0.5, ex, ex - 1) + 127
    byte = np.clip(np.where(amax > 0, byte, 1), 1, 254)
    scaled = (w * np.exp2(127.0 - byte)[:, None, :]).reshape(k, n).astype(np.float32)
    by_word = np.ascontiguousarray(scaled.reshape(k // 512, 128, 4, n).transpose(0, 1, 3, 2))
    if fmt == "e4m3":
        words = by_word.astype(ml_dtypes.float8_e4m3fn).view(np.uint8)
    else:
        c = by_word.astype(ml_dtypes.float4_e2m1fn).view(np.uint8) & 0xF
        words = c[..., 0::2] | (c[..., 1::2] << 4)
    return np.ascontiguousarray(words), np.ascontiguousarray(byte.astype(np.uint8).reshape(k // 512, 16, n))


def unpack_weight(words, scales, fmt):
    g, p, n, _ = words.shape
    if fmt == "e4m3":
        vals = np.ascontiguousarray(words).view(ml_dtypes.float8_e4m3fn).astype(np.float64)
    else:
        nib = np.empty((g, p, n, 4), np.uint8)
        nib[..., 0::2] = words & 0xF
        nib[..., 1::2] = words >> 4
        vals = E2M1[nib]
    vals = vals * np.repeat(np.exp2(scales.astype(np.float64) - 127.0), 8, axis=1)[..., None]
    return vals.transpose(0, 1, 3, 2).reshape(g * 512, n)
def pack4(w):
    words, scales = pack_weight(w, "e2m1")
    return words.reshape(words.shape[0], 128, -1), scales


def unpack4(words, scales):
    return unpack_weight(words.reshape(words.shape[0], 128, -1, 2), scales, "e2m1")


def planes(Y):
    n, m = Y.shape
    b = f64(bf(Y)).reshape(n // 32, 32, m)
    amax = np.abs(b).max(1)
    byte = np.clip(np.where(amax > 0, np.frexp(amax)[1] - 1 + 127 - 7, 1), 1, 254)
    codes = (b * np.exp2(127.0 - byte)[:, None, :]).reshape(n, m).astype(np.float32).astype(ml_dtypes.float8_e4m3fn).view(np.uint8)
    words = codes.reshape(n // 512, 128, 4, m).transpose(0, 1, 3, 2)
    return np.ascontiguousarray(words), np.ascontiguousarray(byte.astype(np.uint8).reshape(n // 512, 16, m))


T, K, C, J, N = 1024, 1024, 512, 4, 2048

def setup_inputs():
    s = mx_kscale(K)[:, None]
    x = np.random.randn(K, T)
    spread = np.exp(0.8 * np.random.randn(N))
    w_gravity = np.random.randn(K, N) / np.sqrt(K) * spread
    w_lever = 1.5 * np.random.randn(K, N) / np.sqrt(K) * spread
    w_load = np.random.randn(K, C) / np.sqrt(K)
    x_words, x_scales = pack_weight(x * s, "e4m3")
    w_gravity_words, w_gravity_scales = pack4(w_gravity / s)
    w_load_words, w_load_scales = pack_weight(w_load / s, "e4m3")
    return {"x_words": x_words, "x_scales": x_scales,
            "w_gravity_words": w_gravity_words, "w_gravity_scales": w_gravity_scales,
            "w_load_words": w_load_words, "w_load_scales": w_load_scales,
            "w_lever": bf(w_lever / s),
            "b_load": bf(0.5 * np.random.randn(C))}

def reference(x_words, x_scales, w_gravity_words, w_gravity_scales, w_load_words, w_load_scales, w_lever, b_load):
    xt = unpack_weight(x_words, x_scales, "e4m3")
    wg = unpack4(w_gravity_words, w_gravity_scales)
    wf = unpack_weight(w_load_words, w_load_scales, "e4m3")
    wl = mxq(f64(w_lever), 0, "e4m3")
    gravity = (xt.T @ wg).reshape(T, C, J)
    lever = (xt.T @ wl).reshape(T, C, J)
    load = 1.0 / (1.0 + np.exp(-((xt.T @ wf) + f64(b_load))))
    y = (gravity + lever * load[:, :, None]).reshape(T, N)
    Y = y.T
    words, scales = planes(Y)
    return y, words, scales

@@ -1,0 +1,306 @@
+from contextlib import ExitStack
+
+import concourse.mybir as mybir
+from concourse.masks import make_identity
+
+T, K, C, J, N = 1024, 1024, 512, 4, 2048
+FLOPS = 2 * T * K * (2 * N + C)
+
+F32 = mybir.dt.float32
+BF16 = mybir.dt.bfloat16
+I32 = mybir.dt.int32
+U32 = mybir.dt.uint32
+U8 = mybir.dt.uint8
+FP8X4 = mybir.dt.float8_e4m3fn_x4
+FP4X4 = mybir.dt.float4_e2m1fn_x4
+ALU = mybir.AluOpType
+ACT = mybir.ActivationFunctionType
+
+P = 128
+PACK = 4
+PASSES = K // (P * PACK)
+BANK = 512
+GROUPS = N // BANK
+ROW_TILES = T // P
+STEPS = GROUPS * ROW_TILES
+HALF = T // 2
+ACC_BANKS = 6
+PIECES = 4
+TURN_LAG = 2
+QUANT_LAG = 5
+
+
+def tile_contact_plan_torques_k3_kernel(
+    tc, x_words, x_scales, w_gravity_words, w_gravity_scales,
+    w_load_words, w_load_scales, w_lever, b_load, out_0, out_1, out_2,
+):
+    nc = tc.nc
+    with ExitStack() as ctx:
+        keep = ctx.enter_context(tc.tile_pool(name="keep", bufs=1))
+        work = ctx.enter_context(tc.tile_pool(name="work", bufs=1))
+        psum = ctx.enter_context(tc.psum_pool(name="psum", bufs=1))
+        ctx.enter_context(tc.manual_schedule())
+
+        x_plane = keep.tile([P, PASSES, T], U8, name="x_plane", align_bytes=64)
+        wf_plane = keep.tile([P, PASSES, C], U8, name="wf_plane", align_bytes=64)
+        wg_plane = keep.tile([P, PASSES, N], U8, name="wg_plane", align_bytes=64)
+        for plane in (x_plane, wf_plane, wg_plane):
+            nc.vector.memset(plane[:].bitcast(I32), 0)
+        ident = keep.tile([P, P], F32, name="ident")
+        make_identity(nc, ident[:])
+
+        def load_plane(plane, scales):
+            for q in range(4):
+                nc.sync.dma_start(
+                    out=plane[32 * q : 32 * q + 4, :, :].bitcast(I32),
+                    in_=scales[:, 4 * q : 4 * q + 4, :].rearrange("g r n -> r g n").bitcast(I32),
+                )
+
+        def load_words(name, rows, lo, hi, dtype, width):
+            tile = keep.tile([P, PASSES, width], dtype, name=name, align_bytes=64)
+            nc.sync.dma_start(out=tile[:].bitcast(I32), in_=rows[:, :, lo:hi].bitcast(I32))
+            return tile
+
+        def load_lever(g, k):
+            raw = keep.tile([P, PACK, BANK], BF16, name="wl_raw%d_%d" % (g, k))
+            rows = w_lever[k * P * PACK : (k + 1) * P * PACK, g * BANK : (g + 1) * BANK]
+            nc.sync.dma_start(out=raw[:], in_=rows.rearrange("(p t) n -> p t n", t=PACK))
+            return raw
+
+        x_rows = x_words.rearrange("g p n t -> p g (n t)")
+        wf_rows = w_load_words.rearrange("g p n t -> p g (n t)")
+        wg_rows = w_gravity_words.rearrange("g p b -> p g b")
+
+        x_codes, wl_raw = {}, {}
+        x_codes[0] = load_words("x_codes0", x_rows, 0, PACK * HALF, U32, HALF)
+        bias_raw = keep.tile([P, PACK], BF16, name="bias_raw")
+        nc.sync.dma_start(out=bias_raw[:], in_=b_load.rearrange("(p j) -> p j", j=PACK))
+        load_plane(x_plane, x_scales)
+        wf_codes = load_words("wf_codes", wf_rows, 0, PACK * C, U32, C)
+        load_plane(wf_plane, w_load_scales)
+        wl_raw[0, 0] = load_lever(0, 0)
+        wl_raw[0, 1] = load_lever(0, 1)
+        x_codes[1] = load_words("x_codes1", x_rows, PACK * HALF, PACK * T, U32, HALF)
+        load_plane(wg_plane, w_gravity_scales)
+        wg_first = load_words("wg_first", wg_rows, 0, 2 * BANK, U8, 2 * BANK)
+        wl_raw[1, 0] = load_lever(1, 0)
+        wl_raw[1, 1] = load_lever(1, 1)
+        wg_rest = load_words("wg_rest", wg_rows, 2 * BANK, 2 * N, U8, 2 * (N - BANK))
+        for g in range(2, GROUPS):
+            for k in range(PASSES):
+                wl_raw[g, k] = load_lever(g, k)
+
+        bias_col = keep.tile([P, PACK], F32, name="bias_col")
+        nc.vector.tensor_copy(out=bias_col[:], in_=bias_raw[:])
+        spread = psum.tile([P, PACK, P], F32, name="spread", tag="turn0")
+        for j in range(PACK):
+            nc.tensor.transpose(spread[:, j, :], bias_col[:, j : j + 1].to_broadcast([P, P]), ident[:])
+        bias_row = keep.tile([P, P, PACK], F32, name="bias_row")
+        nc.vector.tensor_copy(out=bias_row[:], in_=spread[:].rearrange("p j n -> p n j"))
+
+        bank_count = [0]
+
+        def product(row_tile, moving, moving_plane):
+            acc = psum.tile([P, BANK], F32, name="acc", tag="acc%d" % (bank_count[0] % ACC_BANKS))
+            bank_count[0] = bank_count[0] + 1
+            half, at = divmod(row_tile * P, HALF)
+            for k in range(PASSES):
+                nc.tensor.matmul_mx(
+                    out=acc[:],
+                    lhsT=x_codes[half][:, k, at : at + P].bitcast(FP8X4),
+                    lhsT_scale=x_plane[:, k, row_tile * P : (row_tile + 1) * P],
+                    rhs=moving(k),
+                    rhs_scale=moving_plane(k),
+                    start=(k == 0),
+                    stop=(k == PASSES - 1),
+                )
+            return acc
+
+        force, shifted, load = {}, {}, {}
+        grouped, wl_codes, wl_plane = {}, {}, {}
+        lever, gravity, scaled, torque, rounded = {}, {}, {}, {}, {}
+        turned, sorted_words = {}, {}
+
+        def force_product(r):
+            force[r] = product(r, lambda k: wf_codes[:, k, :].bitcast(FP8X4), lambda k: wf_plane[:, k, :])
+
+        def add_bias(r):
+            shifted[r] = work.tile([P, C], F32, name="shifted", bufs=ROW_TILES)
+            nc.vector.tensor_tensor(
+                out=shifted[r][:], in0=force[r][:], in1=bias_row[:].rearrange("p n j -> p (n j)"), op=ALU.add
+            )
+
+        def sigmoid(r):
+            load[r] = keep.tile([P, C], F32, name="load%d" % r)
+            nc.scalar.activation(out=load[r][:], in_=shifted[r][:], func=ACT.Sigmoid)
+
+        def interleave_views(g, k, lo, hi):
+            if (g, k) not in grouped:
+                grouped[g, k] = work.tile([P, BANK, PACK], BF16, name="grouped%d" % k, align_bytes=64)
+            return grouped[g, k][:, lo:hi, :], wl_raw[g, k][:, :, lo:hi].rearrange("p t n -> p n t")
+
+        def interleave_vector(g, k, lo, hi):
+            dst, src = interleave_views(g, k, lo, hi)
+            nc.vector.tensor_copy(out=dst, in_=src)
+
+        def interleave_scalar(g, k, lo, hi):
+            dst, src = interleave_views(g, k, lo, hi)
+            nc.scalar.copy(out=dst, in_=src)
+
+        def interleave_gpsimd(g, k):
+            dst, src = interleave_views(g, k, 0, BANK)
+            nc.gpsimd.tensor_scalar(out=dst, in0=src, scalar1=1.0, scalar2=1.0, op0=ALU.mult, op1=ALU.mult)
+
+        def quantize_lever(g, k):
+            wl_codes[g, k] = keep.tile([P, BANK], U32, name="wl_codes%d_%d" % (g, k), align_bytes=64)
+            wl_plane[g, k] = keep.tile([P, BANK], U8, name="wl_plane%d_%d" % (g, k), align_bytes=64)
+            nc.vector.quantize_mx(
+                out=wl_codes[g, k][:].bitcast(FP8X4),
+                scales=wl_plane[g, k][:],
+                in_=grouped[g, k][:].rearrange("p n t -> p (n t)"),
+            )
+
+        def lever_product(i):
+            g, r = divmod(i, ROW_TILES)
+            lever[i] = product(r, lambda k: wl_codes[g, k][:].bitcast(FP8X4), lambda k: wl_plane[g, k][:])
+
+        def gravity_product(i):
+            g, r = divmod(i, ROW_TILES)
+            words, at = (wg_first, 0) if g == 0 else (wg_rest, 2 * BANK * (g - 1))
+            gravity[i] = product(
+                r,
+                lambda k: words[:, k, at : at + 2 * BANK].bitcast(FP4X4),
+                lambda k: wg_plane[:, k, g * BANK : (g + 1) * BANK],
+            )
+
+        def scale_lever(i):
+            g, r = divmod(i, ROW_TILES)
+            scaled[i] = work.tile([P, P, J], F32, name="scaled", bufs=3)
+            nc.vector.tensor_tensor(
+                out=scaled[i][:],
+                in0=lever[i][:].rearrange("p (c j) -> p c j", j=J),
+                in1=load[r][:, g * P : (g + 1) * P].unsqueeze(2).to_broadcast([P, P, J]),
+                op=ALU.mult,
+            )
+
+        def add_gravity(i):
+            g, r = divmod(i, ROW_TILES)
+            torque[i] = work.tile([P, BANK], F32, name="torque", bufs=12)
+            nc.vector.tensor_tensor(
+                out=torque[i][:], in0=gravity[i][:], in1=scaled[i][:].rearrange("p c j -> p (c j)"), op=ALU.add
+            )
+            nc.sync.dma_start(out=out_0[r * P : (r + 1) * P, g * BANK : (g + 1) * BANK], in_=torque[i][:])
+
+        def round_torque(i):
+            rounded[i] = work.tile([P, BANK], BF16, name="rounded", bufs=8)
+            nc.scalar.copy(
+                out=rounded[i][:].rearrange("p (u m e) -> p u m e", u=2, e=2),
+                in_=torque[i][:].rearrange("p (m u e) -> p u m e", u=2, e=2),
+            )
+
+        turn_count = [0]
+
+        def turn_chunk(first, size):
+            sorted_words[first] = work.tile([P, size * P, 2], F32, name="sorted_words", bufs=3, align_bytes=64)
+            banks = []
+            for lo in range(0, size, 2):
+                pair = min(2, size - lo)
+                bank = psum.tile([P, pair, 2, P], F32, name="turned", tag="turn%d" % (turn_count[0] % 2))
+                turn_count[0] = turn_count[0] + 1
+                for a in range(pair):
+                    words = rounded[first + lo + a][:].bitcast(F32)
+                    for u in range(2):
+                        nc.tensor.transpose(bank[:, a, u, :], words[:, u * P : (u + 1) * P], ident[:])
+                banks.append((lo, pair, bank))
+            for lo, pair, bank in banks:
+                nc.scalar.copy(
+                    out=sorted_words[first][:, lo * P : (lo + pair) * P, :].rearrange("p (a m) u -> p a m u", a=pair),
+                    in_=bank[:].rearrange("p a u m -> p a m u"),
+                )
+
+        y_planes = [keep.tile([P, HALF], U8, name="y_planes%d" % h, align_bytes=64) for h in range(2)]
+        out_words = out_1.rearrange("g p m t -> g p (m t)")
+
+        def quantize_chunk(first, size):
+            g, r = divmod(first, ROW_TILES)
+            half, at = divmod(r * P, HALF)
+            codes = work.tile([P, size * P], U32, name="y_codes", bufs=4, align_bytes=64)
+            nc.vector.quantize_mx(
+                out=codes[:].bitcast(FP8X4),
+                scales=y_planes[half][4 * g : P, at : at + size * P],
+                in_=sorted_words[first][:].rearrange("p m u -> p (m u)").bitcast(BF16),
+            )
+            nc.sync.dma_start(
+                out=out_words[g][:, PACK * r * P : PACK * (r + size) * P].bitcast(I32), in_=codes[:].bitcast(I32)
+            )
+            if g == GROUPS - 1 and at + size * P == HALF:
+                for q in range(4):
+                    queue = nc.scalar if half == 1 and q % 2 == 1 else nc.sync
+                    queue.dma_start(
+                        out=out_2[:, 4 * q : 4 * q + 4, half * HALF : (half + 1) * HALF].bitcast(I32),
+                        in_=y_planes[half][32 * q : 32 * q + 16, :].bitcast(I32),
+                    )
+
+        chunks = [(first, 4) for first in range(0, STEPS - 4, 4)] + [(STEPS - 4, 2), (STEPS - 2, 1), (STEPS - 1, 1)]
+        turn_at = {first + size - 1 + TURN_LAG: (first, size) for first, size in chunks}
+        quant_at = {}
+        for first, size in chunks:
+            lag = QUANT_LAG if first + size < STEPS - 4 else QUANT_LAG - 1
+            quant_at[first + size - 1 + lag] = (first, size)
+
+        width = BANK // PIECES
+        for r in range(ACC_BANKS):
+            force_product(r)
+        interleave_vector(0, 0, 0, BANK // 2)
+        add_bias(0)
+        sigmoid(0)
+        interleave_vector(0, 0, BANK // 2, BANK)
+        interleave_scalar(0, 1, 0, BANK)
+        add_bias(1)
+        quantize_lever(0, 0)
+        force_product(6)
+        force_product(7)
+        add_bias(2)
+        add_bias(3)
+        quantize_lever(0, 1)
+        interleave_gpsimd(1, 1)
+        for r in (1, 2, 3):
+            sigmoid(r)
+        lever_product(0)
+        gravity_product(0)
+        add_bias(4)
+        add_bias(5)
+        lever_product(1)
+        for piece in range(2):
+            interleave_scalar(1, 0, piece * width, (piece + 1) * width)
+
+        for s in range(STEPS + QUANT_LAG):
+            g, r = divmod(s, ROW_TILES)
+            if s < STEPS:
+                scale_lever(s)
+            if s < 2:
+                add_bias(6 + s)
+            if s in quant_at and s < STEPS:
+                quantize_chunk(*quant_at[s])
+            if g + 1 < GROUPS and r == 3:
+                quantize_lever(g + 1, 0)
+            if g + 1 < GROUPS and r == 5:
+                quantize_lever(g + 1, 1)
+                if g + 2 < GROUPS:
+                    interleave_gpsimd(g + 2, 1)
+            if 1 <= s <= STEPS:
+                add_gravity(s - 1)
+                round_torque(s - 1)
+            if s in quant_at and s >= STEPS:
+                quantize_chunk(*quant_at[s])
+            if 2 <= s < 6:
+                sigmoid(2 + s)
+            g2, piece = divmod(s + 2, ROW_TILES)
+            if g2 + 1 < GROUPS and piece < PIECES:
+                interleave_scalar(g2 + 1, 0, piece * width, (piece + 1) * width)
+            if s + 1 < STEPS:
+                gravity_product(s + 1)
+            if s + 2 < STEPS:
+                lever_product(s + 2)
+            if s in turn_at:
+                turn_chunk(*turn_at[s])

@@ -18,16 +18,26 @@ ACT = mybir.ActivationFunctionType
 
 P = 128
 PACK = 4
+QUADRANTS = 4
 PASSES = K // (P * PACK)
 BANK = 512
 GROUPS = N // BANK
 ROW_TILES = T // P
 STEPS = GROUPS * ROW_TILES
 HALF = T // 2
-ACC_BANKS = 6
+
+BATCH = BANK // P
+PRODUCT_BANKS = 6
+SIDE_BANKS = 2
+
+VECTOR_COLUMNS = 320
 PIECES = 4
+PIECE_LEAD = 3
+QUANTIZE_AT = (3, 6)
+FORCE_LEAD = 5
 TURN_LAG = 2
-QUANT_LAG = 5
+PLANES_LAG = 5
+VECTOR_BIAS_BATCHES = 2
 
 
 def tile_contact_plan_torques_k3_kernel(
@@ -43,113 +53,130 @@ def tile_contact_plan_torques_k3_kernel(
 
         x_plane = keep.tile([P, PASSES, T], U8, name="x_plane", align_bytes=64)
         wf_plane = keep.tile([P, PASSES, C], U8, name="wf_plane", align_bytes=64)
-        wg_plane = keep.tile([P, PASSES, N], U8, name="wg_plane", align_bytes=64)
-        for plane in (x_plane, wf_plane, wg_plane):
+        wg_plane_first = keep.tile([P, PASSES, BANK], U8, name="wg_plane_first", align_bytes=64)
+        wg_plane_rest = keep.tile([P, PASSES, N - BANK], U8, name="wg_plane_rest", align_bytes=64)
+        for plane in (x_plane, wg_plane_first, wf_plane, wg_plane_rest):
             nc.vector.memset(plane[:].bitcast(I32), 0)
         ident = keep.tile([P, P], F32, name="ident")
         make_identity(nc, ident[:])
 
-        def load_plane(plane, scales):
-            for q in range(4):
-                nc.sync.dma_start(
-                    out=plane[32 * q : 32 * q + 4, :, :].bitcast(I32),
-                    in_=scales[:, 4 * q : 4 * q + 4, :].rearrange("g r n -> r g n").bitcast(I32),
-                )
+        def load_plane(plane, scales, lo, hi):
+            rows = scales.rearrange("g (q r) n -> r q g n", q=QUADRANTS)
+            for r in range(4):
+                nc.sync.dma_start(out=plane[r:P:32, :, :].bitcast(I32), in_=rows[r][:, :, lo:hi].bitcast(I32))
 
-        def load_words(name, rows, lo, hi, dtype, width):
-            tile = keep.tile([P, PASSES, width], dtype, name=name, align_bytes=64)
-            nc.sync.dma_start(out=tile[:].bitcast(I32), in_=rows[:, :, lo:hi].bitcast(I32))
+        def load_words(name, rows, column_bytes, lo, hi):
+            tile = keep.tile([P, PASSES, column_bytes * (hi - lo)], U8, name=name, align_bytes=64)
+            nc.sync.dma_start(
+                out=tile[:].bitcast(I32), in_=rows[:, :, column_bytes * lo : column_bytes * hi].bitcast(I32)
+            )
             return tile
 
+        wl_raw = {}
+
         def load_lever(g, k):
-            raw = keep.tile([P, PACK, BANK], BF16, name="wl_raw%d_%d" % (g, k))
+            wl_raw[g, k] = keep.tile([P, PACK, BANK], BF16, name="wl_raw%d_%d" % (g, k))
             rows = w_lever[k * P * PACK : (k + 1) * P * PACK, g * BANK : (g + 1) * BANK]
-            nc.sync.dma_start(out=raw[:], in_=rows.rearrange("(p t) n -> p t n", t=PACK))
-            return raw
+            nc.sync.dma_start(out=wl_raw[g, k][:], in_=rows.rearrange("(p t) n -> p t n", t=PACK))
 
         x_rows = x_words.rearrange("g p n t -> p g (n t)")
         wf_rows = w_load_words.rearrange("g p n t -> p g (n t)")
         wg_rows = w_gravity_words.rearrange("g p b -> p g b")
 
-        x_codes, wl_raw = {}, {}
-        x_codes[0] = load_words("x_codes0", x_rows, 0, PACK * HALF, U32, HALF)
+        load_lever(0, 0)
         bias_raw = keep.tile([P, PACK], BF16, name="bias_raw")
-        nc.sync.dma_start(out=bias_raw[:], in_=b_load.rearrange("(p j) -> p j", j=PACK))
-        load_plane(x_plane, x_scales)
-        wf_codes = load_words("wf_codes", wf_rows, 0, PACK * C, U32, C)
-        load_plane(wf_plane, w_load_scales)
-        wl_raw[0, 0] = load_lever(0, 0)
-        wl_raw[0, 1] = load_lever(0, 1)
-        x_codes[1] = load_words("x_codes1", x_rows, PACK * HALF, PACK * T, U32, HALF)
-        load_plane(wg_plane, w_gravity_scales)
-        wg_first = load_words("wg_first", wg_rows, 0, 2 * BANK, U8, 2 * BANK)
-        wl_raw[1, 0] = load_lever(1, 0)
-        wl_raw[1, 1] = load_lever(1, 1)
-        wg_rest = load_words("wg_rest", wg_rows, 2 * BANK, 2 * N, U8, 2 * (N - BANK))
+        nc.sync.dma_start(out=bias_raw[:], in_=b_load.rearrange("(p i) -> p i", i=PACK))
+        load_plane(x_plane, x_scales, 0, T)
+        load_lever(0, 1)
+        x_first = load_words("x_first", x_rows, 4, 0, HALF)
+        load_plane(wf_plane, w_load_scales, 0, C)
+        wf_first = load_words("wf_first", wf_rows, 4, 0, P)
+        load_plane(wg_plane_first, w_gravity_scales, 0, BANK)
+        wg_first = load_words("wg_first", wg_rows, 2, 0, BANK)
+        x_second = load_words("x_second", x_rows, 4, HALF, T)
+        load_lever(1, 0)
+        load_lever(1, 1)
+        wf_rest = load_words("wf_rest", wf_rows, 4, P, C)
+        load_plane(wg_plane_rest, w_gravity_scales, BANK, N)
+        wg_rest = load_words("wg_rest", wg_rows, 2, BANK, N)
         for g in range(2, GROUPS):
             for k in range(PASSES):
-                wl_raw[g, k] = load_lever(g, k)
+                load_lever(g, k)
 
-        bias_col = keep.tile([P, PACK], F32, name="bias_col")
-        nc.vector.tensor_copy(out=bias_col[:], in_=bias_raw[:])
-        spread = psum.tile([P, PACK, P], F32, name="spread", tag="turn0")
-        for j in range(PACK):
-            nc.tensor.transpose(spread[:, j, :], bias_col[:, j : j + 1].to_broadcast([P, P]), ident[:])
-        bias_row = keep.tile([P, P, PACK], F32, name="bias_row")
-        nc.vector.tensor_copy(out=bias_row[:], in_=spread[:].rearrange("p j n -> p n j"))
+        product_banks, side_banks = [], []
 
-        bank_count = [0]
+        def next_bank(taken, kind, count, shape):
+            bank = psum.tile(shape, F32, name=kind, tag="%s%d" % (kind, len(taken) % count))
+            taken.append(bank)
+            return bank
 
-        def product(row_tile, moving, moving_plane):
-            acc = psum.tile([P, BANK], F32, name="acc", tag="acc%d" % (bank_count[0] % ACC_BANKS))
-            bank_count[0] = bank_count[0] + 1
+        def next_product_bank():
+            return next_bank(product_banks, "product", PRODUCT_BANKS, [P, BANK])
+
+        def next_side_bank(shape):
+            return next_bank(side_banks, "side", SIDE_BANKS, shape)
+
+        force, shifted, load = {}, {}, {}
+        grouped, wl_codes, wl_plane = {}, {}, {}
+        lever, gravity, scaled, torque, rounded = {}, {}, {}, {}, {}
+        pair_words = {}
+
+        def product(acc, row_tile, moving, moving_plane):
             half, at = divmod(row_tile * P, HALF)
+            x_codes = (x_first, x_second)[half]
             for k in range(PASSES):
                 nc.tensor.matmul_mx(
-                    out=acc[:],
-                    lhsT=x_codes[half][:, k, at : at + P].bitcast(FP8X4),
+                    out=acc,
+                    lhsT=x_codes[:, k, 4 * at : 4 * (at + P)].bitcast(FP8X4),
                     lhsT_scale=x_plane[:, k, row_tile * P : (row_tile + 1) * P],
                     rhs=moving(k),
                     rhs_scale=moving_plane(k),
                     start=(k == 0),
                     stop=(k == PASSES - 1),
                 )
-            return acc
 
-        force, shifted, load = {}, {}, {}
-        grouped, wl_codes, wl_plane = {}, {}, {}
-        lever, gravity, scaled, torque, rounded = {}, {}, {}, {}, {}
-        turned, sorted_words = {}, {}
+        def force_product(b):
+            g, first_row_tile = divmod(b * BATCH, ROW_TILES)
+            words, at = (wf_first, 0) if g == 0 else (wf_rest, P * (g - 1))
+            force[b] = next_side_bank([P, BATCH, P])
+            for a in range(BATCH):
+                product(
+                    force[b][:, a, :],
+                    first_row_tile + a,
+                    lambda k: words[:, k, 4 * at : 4 * (at + P)].bitcast(FP8X4),
+                    lambda k: wf_plane[:, k, g * P : (g + 1) * P],
+                )
 
-        def force_product(r):
-            force[r] = product(r, lambda k: wf_codes[:, k, :].bitcast(FP8X4), lambda k: wf_plane[:, k, :])
-
-        def add_bias(r):
-            shifted[r] = work.tile([P, C], F32, name="shifted", bufs=ROW_TILES)
-            nc.vector.tensor_tensor(
-                out=shifted[r][:], in0=force[r][:], in1=bias_row[:].rearrange("p n j -> p (n j)"), op=ALU.add
+        def add_bias(b):
+            g = b * BATCH // ROW_TILES
+            shifted[b] = work.tile([P, BATCH, P], F32, name="shifted", bufs=2)
+            bias = bias_row[:].rearrange("p m i -> p (m i)")[:, g * P : (g + 1) * P]
+            source, engine = force[b], nc.vector
+            if b >= VECTOR_BIAS_BATCHES:
+                source, engine = work.tile([P, BATCH, P], F32, name="force_copy", bufs=2), nc.gpsimd
+                nc.scalar.copy(out=source[:], in_=force[b][:])
+            engine.tensor_tensor(
+                out=shifted[b][:], in0=source[:], in1=bias.unsqueeze(1).to_broadcast([P, BATCH, P]), op=ALU.add
             )
 
-        def sigmoid(r):
-            load[r] = keep.tile([P, C], F32, name="load%d" % r)
-            nc.scalar.activation(out=load[r][:], in_=shifted[r][:], func=ACT.Sigmoid)
+        def sigmoid(b):
+            load[b] = work.tile([P, BATCH, P], F32, name="load", bufs=4)
+            nc.scalar.activation(out=load[b][:], in_=shifted[b][:], func=ACT.Sigmoid)
 
         def interleave_views(g, k, lo, hi):
             if (g, k) not in grouped:
                 grouped[g, k] = work.tile([P, BANK, PACK], BF16, name="grouped%d" % k, align_bytes=64)
-            return grouped[g, k][:, lo:hi, :], wl_raw[g, k][:, :, lo:hi].rearrange("p t n -> p n t")
+            return grouped[g, k][:, lo:hi, :], wl_raw[g, k][:, :, lo:hi]
 
-        def interleave_vector(g, k, lo, hi):
+        def interleave(copy, g, k, lo, hi):
             dst, src = interleave_views(g, k, lo, hi)
-            nc.vector.tensor_copy(out=dst, in_=src)
-
-        def interleave_scalar(g, k, lo, hi):
-            dst, src = interleave_views(g, k, lo, hi)
-            nc.scalar.copy(out=dst, in_=src)
+            copy(out=dst.rearrange("p (c i) t -> p c t i", i=4), in_=src.rearrange("p t (c i) -> p c t i", i=4))
 
         def interleave_gpsimd(g, k):
             dst, src = interleave_views(g, k, 0, BANK)
-            nc.gpsimd.tensor_scalar(out=dst, in0=src, scalar1=1.0, scalar2=1.0, op0=ALU.mult, op1=ALU.mult)
+            nc.gpsimd.tensor_scalar(
+                out=dst, in0=src.rearrange("p t n -> p n t"), scalar1=1.0, scalar2=1.0, op0=ALU.mult, op1=ALU.mult
+            )
 
         def quantize_lever(g, k):
             wl_codes[g, k] = keep.tile([P, BANK], U32, name="wl_codes%d_%d" % (g, k), align_bytes=64)
@@ -160,147 +187,150 @@ def tile_contact_plan_torques_k3_kernel(
                 in_=grouped[g, k][:].rearrange("p n t -> p (n t)"),
             )
 
-        def lever_product(i):
-            g, r = divmod(i, ROW_TILES)
-            lever[i] = product(r, lambda k: wl_codes[g, k][:].bitcast(FP8X4), lambda k: wl_plane[g, k][:])
+        def lever_product(s):
+            g, r = divmod(s, ROW_TILES)
+            lever[s] = next_product_bank()
+            product(lever[s][:], r, lambda k: wl_codes[g, k][:].bitcast(FP8X4), lambda k: wl_plane[g, k][:])
 
-        def gravity_product(i):
-            g, r = divmod(i, ROW_TILES)
-            words, at = (wg_first, 0) if g == 0 else (wg_rest, 2 * BANK * (g - 1))
-            gravity[i] = product(
+        def gravity_product(s):
+            g, r = divmod(s, ROW_TILES)
+            words, plane, at = (wg_first, wg_plane_first, 0) if g == 0 else (wg_rest, wg_plane_rest, BANK * (g - 1))
+            gravity[s] = next_product_bank()
+            product(
+                gravity[s][:],
                 r,
-                lambda k: words[:, k, at : at + 2 * BANK].bitcast(FP4X4),
-                lambda k: wg_plane[:, k, g * BANK : (g + 1) * BANK],
+                lambda k: words[:, k, 2 * at : 2 * (at + BANK)].bitcast(FP4X4),
+                lambda k: plane[:, k, at : at + BANK],
             )
 
-        def scale_lever(i):
-            g, r = divmod(i, ROW_TILES)
-            scaled[i] = work.tile([P, P, J], F32, name="scaled", bufs=3)
+        def scale_lever(s):
+            scaled[s] = work.tile([P, P, J], F32, name="scaled", bufs=3)
             nc.vector.tensor_tensor(
-                out=scaled[i][:],
-                in0=lever[i][:].rearrange("p (c j) -> p c j", j=J),
-                in1=load[r][:, g * P : (g + 1) * P].unsqueeze(2).to_broadcast([P, P, J]),
+                out=scaled[s][:],
+                in0=lever[s][:].rearrange("p (c j) -> p c j", j=J),
+                in1=load[s // BATCH][:, s % BATCH, :].unsqueeze(2).to_broadcast([P, P, J]),
                 op=ALU.mult,
             )
 
-        def add_gravity(i):
-            g, r = divmod(i, ROW_TILES)
-            torque[i] = work.tile([P, BANK], F32, name="torque", bufs=12)
+        def add_gravity(s):
+            g, r = divmod(s, ROW_TILES)
+            torque[s] = work.tile([P, BANK], F32, name="torque", bufs=12)
             nc.vector.tensor_tensor(
-                out=torque[i][:], in0=gravity[i][:], in1=scaled[i][:].rearrange("p c j -> p (c j)"), op=ALU.add
+                out=torque[s][:], in0=gravity[s][:], in1=scaled[s][:].rearrange("p c j -> p (c j)"), op=ALU.add
             )
-            nc.sync.dma_start(out=out_0[r * P : (r + 1) * P, g * BANK : (g + 1) * BANK], in_=torque[i][:])
+            nc.sync.dma_start(out=out_0[r * P : (r + 1) * P, g * BANK : (g + 1) * BANK], in_=torque[s][:])
 
-        def round_torque(i):
-            rounded[i] = work.tile([P, BANK], BF16, name="rounded", bufs=8)
-            nc.scalar.copy(
-                out=rounded[i][:].rearrange("p (u m e) -> p u m e", u=2, e=2),
-                in_=torque[i][:].rearrange("p (m u e) -> p u m e", u=2, e=2),
+        def round_torque(s, copy):
+            rounded[s] = work.tile([P, BANK], BF16, name="rounded", bufs=2 * BATCH)
+            copy(
+                out=rounded[s][:].rearrange("p (u m e) -> p u m e", u=2, e=2),
+                in_=torque[s][:].rearrange("p (m u e) -> p u m e", u=2, e=2),
             )
 
-        turn_count = [0]
-
-        def turn_chunk(first, size):
-            sorted_words[first] = work.tile([P, size * P, 2], F32, name="sorted_words", bufs=3, align_bytes=64)
+        def turn(first, size):
+            pair_words[first] = work.tile([P, size * P, 2], F32, name="pair_words", bufs=3, align_bytes=64)
             banks = []
             for lo in range(0, size, 2):
-                pair = min(2, size - lo)
-                bank = psum.tile([P, pair, 2, P], F32, name="turned", tag="turn%d" % (turn_count[0] % 2))
-                turn_count[0] = turn_count[0] + 1
-                for a in range(pair):
-                    words = rounded[first + lo + a][:].bitcast(F32)
+                banks.append(next_side_bank([P, 2, 2, P]))
+                for a in range(2):
+                    pairs = rounded[first + lo + a][:].bitcast(F32)
                     for u in range(2):
-                        nc.tensor.transpose(bank[:, a, u, :], words[:, u * P : (u + 1) * P], ident[:])
-                banks.append((lo, pair, bank))
-            for lo, pair, bank in banks:
+                        nc.tensor.transpose(banks[-1][:, a, u, :], pairs[:, u * P : (u + 1) * P], ident[:])
+            return banks
+
+        def empty_turned(first, banks):
+            for n, bank in enumerate(banks):
                 nc.scalar.copy(
-                    out=sorted_words[first][:, lo * P : (lo + pair) * P, :].rearrange("p (a m) u -> p a m u", a=pair),
+                    out=pair_words[first][:, 2 * n * P : 2 * (n + 1) * P, :].rearrange("p (a m) u -> p a m u", a=2),
                     in_=bank[:].rearrange("p a u m -> p a m u"),
                 )
 
-        y_planes = [keep.tile([P, HALF], U8, name="y_planes%d" % h, align_bytes=64) for h in range(2)]
+        y_planes = keep.tile([P, T], U8, name="y_planes", align_bytes=64)
         out_words = out_1.rearrange("g p m t -> g p (m t)")
 
-        def quantize_chunk(first, size):
+        def quantize_torque(first, size):
             g, r = divmod(first, ROW_TILES)
-            half, at = divmod(r * P, HALF)
             codes = work.tile([P, size * P], U32, name="y_codes", bufs=4, align_bytes=64)
             nc.vector.quantize_mx(
                 out=codes[:].bitcast(FP8X4),
-                scales=y_planes[half][4 * g : P, at : at + size * P],
-                in_=sorted_words[first][:].rearrange("p m u -> p (m u)").bitcast(BF16),
+                scales=y_planes[4 * g : P, r * P : (r + size) * P],
+                in_=pair_words[first][:].rearrange("p m u -> p (m u)").bitcast(BF16),
             )
             nc.sync.dma_start(
                 out=out_words[g][:, PACK * r * P : PACK * (r + size) * P].bitcast(I32), in_=codes[:].bitcast(I32)
             )
-            if g == GROUPS - 1 and at + size * P == HALF:
-                for q in range(4):
-                    queue = nc.scalar if half == 1 and q % 2 == 1 else nc.sync
-                    queue.dma_start(
-                        out=out_2[:, 4 * q : 4 * q + 4, half * HALF : (half + 1) * HALF].bitcast(I32),
-                        in_=y_planes[half][32 * q : 32 * q + 16, :].bitcast(I32),
-                    )
 
-        chunks = [(first, 4) for first in range(0, STEPS - 4, 4)] + [(STEPS - 4, 2), (STEPS - 2, 1), (STEPS - 1, 1)]
-        turn_at = {first + size - 1 + TURN_LAG: (first, size) for first, size in chunks}
-        quant_at = {}
-        for first, size in chunks:
-            lag = QUANT_LAG if first + size < STEPS - 4 else QUANT_LAG - 1
-            quant_at[first + size - 1 + lag] = (first, size)
+        bias_col = keep.tile([P, PACK], F32, name="bias_col")
+        nc.scalar.copy(out=bias_col[:], in_=bias_raw[:])
+        spread = next_side_bank([P, PACK, P])
+        for i in range(PACK):
+            nc.tensor.transpose(spread[:, i, :], bias_col[:, i : i + 1].to_broadcast([P, P]), ident[:])
+        bias_row = keep.tile([P, P, PACK], F32, name="bias_row")
 
-        width = BANK // PIECES
-        for r in range(ACC_BANKS):
-            force_product(r)
-        interleave_vector(0, 0, 0, BANK // 2)
-        add_bias(0)
-        sigmoid(0)
-        interleave_vector(0, 0, BANK // 2, BANK)
-        interleave_scalar(0, 1, 0, BANK)
-        add_bias(1)
+        interleave(nc.scalar.copy, 0, 0, VECTOR_COLUMNS, BANK)
+        interleave(nc.vector.tensor_copy, 0, 0, 0, VECTOR_COLUMNS)
+        nc.scalar.copy(out=bias_row[:], in_=spread[:].rearrange("p i m -> p m i"))
+        interleave(nc.scalar.copy, 0, 1, VECTOR_COLUMNS, BANK)
+        interleave(nc.vector.tensor_copy, 0, 1, 0, VECTOR_COLUMNS)
         quantize_lever(0, 0)
-        force_product(6)
-        force_product(7)
-        add_bias(2)
-        add_bias(3)
         quantize_lever(0, 1)
         interleave_gpsimd(1, 1)
-        for r in (1, 2, 3):
-            sigmoid(r)
+        force_product(0)
+        add_bias(0)
+        sigmoid(0)
         lever_product(0)
         gravity_product(0)
-        add_bias(4)
-        add_bias(5)
         lever_product(1)
-        for piece in range(2):
-            interleave_scalar(1, 0, piece * width, (piece + 1) * width)
 
-        for s in range(STEPS + QUANT_LAG):
+        force_at = {max(BATCH * b - FORCE_LEAD, 0): b for b in range(1, STEPS // BATCH)}
+        piece_at = {}
+        for g in range(1, GROUPS):
+            for piece in range(PIECES):
+                piece_at.setdefault(max((g - 1) * ROW_TILES - PIECE_LEAD + piece, 0), []).append((g, piece))
+        width = BANK // PIECES
+
+        for s in range(STEPS):
             g, r = divmod(s, ROW_TILES)
-            if s < STEPS:
-                scale_lever(s)
-            if s < 2:
-                add_bias(6 + s)
-            if s in quant_at and s < STEPS:
-                quantize_chunk(*quant_at[s])
-            if g + 1 < GROUPS and r == 3:
+            scale_lever(s)
+            if s - 1 in force_at:
+                add_bias(force_at[s - 1])
+            if g + 1 < GROUPS and r == QUANTIZE_AT[0]:
                 quantize_lever(g + 1, 0)
-            if g + 1 < GROUPS and r == 5:
+            if s >= 1:
+                add_gravity(s - 1)
+                round_torque(s - 1, nc.scalar.copy)
+            if s - 2 in force_at:
+                sigmoid(force_at[s - 2])
+            to_quantize = s - PLANES_LAG - (BATCH - 1)
+            if to_quantize >= 0 and to_quantize % BATCH == 0:
+                quantize_torque(to_quantize, BATCH)
+            if g + 1 < GROUPS and r == QUANTIZE_AT[1]:
                 quantize_lever(g + 1, 1)
                 if g + 2 < GROUPS:
                     interleave_gpsimd(g + 2, 1)
-            if 1 <= s <= STEPS:
-                add_gravity(s - 1)
-                round_torque(s - 1)
-            if s in quant_at and s >= STEPS:
-                quantize_chunk(*quant_at[s])
-            if 2 <= s < 6:
-                sigmoid(2 + s)
-            g2, piece = divmod(s + 2, ROW_TILES)
-            if g2 + 1 < GROUPS and piece < PIECES:
-                interleave_scalar(g2 + 1, 0, piece * width, (piece + 1) * width)
+            for next_group, piece in piece_at.get(s, []):
+                interleave(nc.scalar.copy, next_group, 0, piece * width, (piece + 1) * width)
             if s + 1 < STEPS:
                 gravity_product(s + 1)
+            if s in force_at:
+                force_product(force_at[s])
             if s + 2 < STEPS:
                 lever_product(s + 2)
-            if s in turn_at:
-                turn_chunk(*turn_at[s])
+            to_turn = s - TURN_LAG - (BATCH - 1)
+            if to_turn >= 0 and to_turn % BATCH == 0:
+                empty_turned(to_turn, turn(to_turn, BATCH))
+
+        last = STEPS - BATCH
+        empty_turned(last, turn(last, 2))
+        add_gravity(STEPS - 1)
+        round_torque(STEPS - 1, nc.vector.tensor_copy)
+        quantize_torque(last - BATCH, BATCH)
+        final_banks = turn(last + 2, 2)
+        quantize_torque(last, 2)
+        empty_turned(last + 2, final_banks)
+        quantize_torque(last + 2, 2)
+        for q in range(QUADRANTS):
+            queue = (nc.sync, nc.scalar)[q % 2]
+            queue.dma_start(
+                out=out_2[:, 4 * q : 4 * q + 4, :].bitcast(I32), in_=y_planes[32 * q : 32 * q + 16, :].bitcast(I32)
+            )

@@ -30,13 +30,15 @@ BATCH = BANK // P
 PRODUCT_BANKS = 6
 SIDE_BANKS = 2
 
+WF_PLANE_START = 4
+
 VECTOR_COLUMNS = 320
-PIECES = 4
-PIECE_LEAD = 3
+PIECES = 2
+PIECE_LEAD = 1
 QUANTIZE_AT = (3, 6)
 FORCE_LEAD = 5
 TURN_LAG = 2
-PLANES_LAG = 5
+PLANES_LAG = 7
 VECTOR_BIAS_BATCHES = 2
 
 
@@ -60,10 +62,12 @@ def tile_contact_plan_torques_k3_kernel(
         ident = keep.tile([P, P], F32, name="ident")
         make_identity(nc, ident[:])
 
-        def load_plane(plane, scales, lo, hi):
+        def load_plane(plane, scales, lo, hi, start=0):
             rows = scales.rearrange("g (q r) n -> r q g n", q=QUADRANTS)
             for r in range(4):
-                nc.sync.dma_start(out=plane[r:P:32, :, :].bitcast(I32), in_=rows[r][:, :, lo:hi].bitcast(I32))
+                nc.sync.dma_start(
+                    out=plane[start + r : P : 32, :, :].bitcast(I32), in_=rows[r][:, :, lo:hi].bitcast(I32)
+                )
 
         def load_words(name, rows, column_bytes, lo, hi):
             tile = keep.tile([P, PASSES, column_bytes * (hi - lo)], U8, name=name, align_bytes=64)
@@ -87,13 +91,13 @@ def tile_contact_plan_torques_k3_kernel(
         bias_raw = keep.tile([P, PACK], BF16, name="bias_raw")
         nc.sync.dma_start(out=bias_raw[:], in_=b_load.rearrange("(p i) -> p i", i=PACK))
         load_plane(x_plane, x_scales, 0, T)
-        load_lever(0, 1)
         x_first = load_words("x_first", x_rows, 4, 0, HALF)
-        load_plane(wf_plane, w_load_scales, 0, C)
+        load_lever(0, 1)
+        load_plane(wf_plane, w_load_scales, 0, C, WF_PLANE_START)
         wf_first = load_words("wf_first", wf_rows, 4, 0, P)
-        load_plane(wg_plane_first, w_gravity_scales, 0, BANK)
         wg_first = load_words("wg_first", wg_rows, 2, 0, BANK)
         x_second = load_words("x_second", x_rows, 4, HALF, T)
+        load_plane(wg_plane_first, w_gravity_scales, 0, BANK)
         load_lever(1, 0)
         load_lever(1, 1)
         wf_rest = load_words("wf_rest", wf_rows, 4, P, C)
@@ -121,10 +125,10 @@ def tile_contact_plan_torques_k3_kernel(
         lever, gravity, scaled, torque, rounded = {}, {}, {}, {}, {}
         pair_words = {}
 
-        def product(acc, row_tile, moving, moving_plane):
+        def product(acc, row_tile, moving, moving_plane, passes=range(PASSES)):
             half, at = divmod(row_tile * P, HALF)
             x_codes = (x_first, x_second)[half]
-            for k in range(PASSES):
+            for k in passes:
                 nc.tensor.matmul_mx(
                     out=acc,
                     lhsT=x_codes[:, k, 4 * at : 4 * (at + P)].bitcast(FP8X4),
@@ -144,7 +148,7 @@ def tile_contact_plan_torques_k3_kernel(
                     force[b][:, a, :],
                     first_row_tile + a,
                     lambda k: words[:, k, 4 * at : 4 * (at + P)].bitcast(FP8X4),
-                    lambda k: wf_plane[:, k, g * P : (g + 1) * P],
+                    lambda k: wf_plane[WF_PLANE_START:P, k, g * P : (g + 1) * P],
                 )
 
         def add_bias(b):
@@ -187,10 +191,11 @@ def tile_contact_plan_torques_k3_kernel(
                 in_=grouped[g, k][:].rearrange("p n t -> p (n t)"),
             )
 
-        def lever_product(s):
+        def lever_product(s, passes=range(PASSES)):
             g, r = divmod(s, ROW_TILES)
-            lever[s] = next_product_bank()
-            product(lever[s][:], r, lambda k: wl_codes[g, k][:].bitcast(FP8X4), lambda k: wl_plane[g, k][:])
+            if s not in lever:
+                lever[s] = next_product_bank()
+            product(lever[s][:], r, lambda k: wl_codes[g, k][:].bitcast(FP8X4), lambda k: wl_plane[g, k][:], passes)
 
         def gravity_product(s):
             g, r = divmod(s, ROW_TILES)
@@ -270,17 +275,19 @@ def tile_contact_plan_torques_k3_kernel(
         interleave(nc.scalar.copy, 0, 0, VECTOR_COLUMNS, BANK)
         interleave(nc.vector.tensor_copy, 0, 0, 0, VECTOR_COLUMNS)
         nc.scalar.copy(out=bias_row[:], in_=spread[:].rearrange("p i m -> p m i"))
+        quantize_lever(0, 0)
+        lever_product(0, [0])
+        lever_product(1, [0])
+        force_product(0)
         interleave(nc.scalar.copy, 0, 1, VECTOR_COLUMNS, BANK)
         interleave(nc.vector.tensor_copy, 0, 1, 0, VECTOR_COLUMNS)
-        quantize_lever(0, 0)
         quantize_lever(0, 1)
         interleave_gpsimd(1, 1)
-        force_product(0)
         add_bias(0)
         sigmoid(0)
-        lever_product(0)
+        lever_product(0, [1])
         gravity_product(0)
-        lever_product(1)
+        lever_product(1, [1])
 
         force_at = {max(BATCH * b - FORCE_LEAD, 0): b for b in range(1, STEPS // BATCH)}
         piece_at = {}

from contextlib import ExitStack

import concourse.mybir as mybir
from concourse.masks import make_identity

T, K, C, J, N = 1024, 1024, 512, 4, 2048
FLOPS = 2 * T * K * (2 * N + C)

F32 = mybir.dt.float32
BF16 = mybir.dt.bfloat16
I32 = mybir.dt.int32
U32 = mybir.dt.uint32
U8 = mybir.dt.uint8
FP8X4 = mybir.dt.float8_e4m3fn_x4
FP4X4 = mybir.dt.float4_e2m1fn_x4
ALU = mybir.AluOpType
ACT = mybir.ActivationFunctionType

P = 128
PACK = 4
QUADRANTS = 4
PASSES = K // (P * PACK)
BANK = 512
GROUPS = N // BANK
ROW_TILES = T // P
STEPS = GROUPS * ROW_TILES
HALF = T // 2

BATCH = BANK // P
PRODUCT_BANKS = 6
SIDE_BANKS = 2

WF_PLANE_START = 4

VECTOR_COLUMNS = 320
PIECES = 2
PIECE_LEAD = 1
QUANTIZE_AT = (3, 6)
FORCE_LEAD = 5
TURN_LAG = 2
PLANES_LAG = 7
VECTOR_BIAS_BATCHES = 2


def tile_contact_plan_torques_k3_kernel(
    tc, x_words, x_scales, w_gravity_words, w_gravity_scales,
    w_load_words, w_load_scales, w_lever, b_load, out_0, out_1, out_2,
):
    nc = tc.nc
    with ExitStack() as ctx:
        keep = ctx.enter_context(tc.tile_pool(name="keep", bufs=1))
        work = ctx.enter_context(tc.tile_pool(name="work", bufs=1))
        psum = ctx.enter_context(tc.psum_pool(name="psum", bufs=1))
        ctx.enter_context(tc.manual_schedule())

        x_plane = keep.tile([P, PASSES, T], U8, name="x_plane", align_bytes=64)
        wf_plane = keep.tile([P, PASSES, C], U8, name="wf_plane", align_bytes=64)
        wg_plane_first = keep.tile([P, PASSES, BANK], U8, name="wg_plane_first", align_bytes=64)
        wg_plane_rest = keep.tile([P, PASSES, N - BANK], U8, name="wg_plane_rest", align_bytes=64)
        for plane in (x_plane, wg_plane_first, wf_plane, wg_plane_rest):
            nc.vector.memset(plane[:].bitcast(I32), 0)
        ident = keep.tile([P, P], F32, name="ident")
        make_identity(nc, ident[:])

        def load_plane(plane, scales, lo, hi, start=0):
            rows = scales.rearrange("g (q r) n -> r q g n", q=QUADRANTS)
            for r in range(4):
                nc.sync.dma_start(
                    out=plane[start + r : P : 32, :, :].bitcast(I32), in_=rows[r][:, :, lo:hi].bitcast(I32)
                )

        def load_words(name, rows, column_bytes, lo, hi):
            tile = keep.tile([P, PASSES, column_bytes * (hi - lo)], U8, name=name, align_bytes=64)
            nc.sync.dma_start(
                out=tile[:].bitcast(I32), in_=rows[:, :, column_bytes * lo : column_bytes * hi].bitcast(I32)
            )
            return tile

        wl_raw = {}

        def load_lever(g, k):
            wl_raw[g, k] = keep.tile([P, PACK, BANK], BF16, name="wl_raw%d_%d" % (g, k))
            rows = w_lever[k * P * PACK : (k + 1) * P * PACK, g * BANK : (g + 1) * BANK]
            nc.sync.dma_start(out=wl_raw[g, k][:], in_=rows.rearrange("(p t) n -> p t n", t=PACK))

        x_rows = x_words.rearrange("g p n t -> p g (n t)")
        wf_rows = w_load_words.rearrange("g p n t -> p g (n t)")
        wg_rows = w_gravity_words.rearrange("g p b -> p g b")

        load_lever(0, 0)
        bias_raw = keep.tile([P, PACK], BF16, name="bias_raw")
        nc.sync.dma_start(out=bias_raw[:], in_=b_load.rearrange("(p i) -> p i", i=PACK))
        load_plane(x_plane, x_scales, 0, T)
        x_first = load_words("x_first", x_rows, 4, 0, HALF)
        load_lever(0, 1)
        load_plane(wf_plane, w_load_scales, 0, C, WF_PLANE_START)
        wf_first = load_words("wf_first", wf_rows, 4, 0, P)
        wg_first = load_words("wg_first", wg_rows, 2, 0, BANK)
        x_second = load_words("x_second", x_rows, 4, HALF, T)
        load_plane(wg_plane_first, w_gravity_scales, 0, BANK)
        load_lever(1, 0)
        load_lever(1, 1)
        wf_rest = load_words("wf_rest", wf_rows, 4, P, C)
        load_plane(wg_plane_rest, w_gravity_scales, BANK, N)
        wg_rest = load_words("wg_rest", wg_rows, 2, BANK, N)
        for g in range(2, GROUPS):
            for k in range(PASSES):
                load_lever(g, k)

        product_banks, side_banks = [], []

        def next_bank(taken, kind, count, shape):
            bank = psum.tile(shape, F32, name=kind, tag="%s%d" % (kind, len(taken) % count))
            taken.append(bank)
            return bank

        def next_product_bank():
            return next_bank(product_banks, "product", PRODUCT_BANKS, [P, BANK])

        def next_side_bank(shape):
            return next_bank(side_banks, "side", SIDE_BANKS, shape)

        force, shifted, load = {}, {}, {}
        grouped, wl_codes, wl_plane = {}, {}, {}
        lever, gravity, scaled, torque, rounded = {}, {}, {}, {}, {}
        pair_words = {}

        def product(acc, row_tile, moving, moving_plane, passes=range(PASSES)):
            half, at = divmod(row_tile * P, HALF)
            x_codes = (x_first, x_second)[half]
            for k in passes:
                nc.tensor.matmul_mx(
                    out=acc,
                    lhsT=x_codes[:, k, 4 * at : 4 * (at + P)].bitcast(FP8X4),
                    lhsT_scale=x_plane[:, k, row_tile * P : (row_tile + 1) * P],
                    rhs=moving(k),
                    rhs_scale=moving_plane(k),
                    start=(k == 0),
                    stop=(k == PASSES - 1),
                )

        def force_product(b):
            g, first_row_tile = divmod(b * BATCH, ROW_TILES)
            words, at = (wf_first, 0) if g == 0 else (wf_rest, P * (g - 1))
            force[b] = next_side_bank([P, BATCH, P])
            for a in range(BATCH):
                product(
                    force[b][:, a, :],
                    first_row_tile + a,
                    lambda k: words[:, k, 4 * at : 4 * (at + P)].bitcast(FP8X4),
                    lambda k: wf_plane[WF_PLANE_START:P, k, g * P : (g + 1) * P],
                )

        def add_bias(b):
            g = b * BATCH // ROW_TILES
            shifted[b] = work.tile([P, BATCH, P], F32, name="shifted", bufs=2)
            bias = bias_row[:].rearrange("p m i -> p (m i)")[:, g * P : (g + 1) * P]
            source, engine = force[b], nc.vector
            if b >= VECTOR_BIAS_BATCHES:
                source, engine = work.tile([P, BATCH, P], F32, name="force_copy", bufs=2), nc.gpsimd
                nc.scalar.copy(out=source[:], in_=force[b][:])
            engine.tensor_tensor(
                out=shifted[b][:], in0=source[:], in1=bias.unsqueeze(1).to_broadcast([P, BATCH, P]), op=ALU.add
            )

        def sigmoid(b):
            load[b] = work.tile([P, BATCH, P], F32, name="load", bufs=4)
            nc.scalar.activation(out=load[b][:], in_=shifted[b][:], func=ACT.Sigmoid)

        def interleave_views(g, k, lo, hi):
            if (g, k) not in grouped:
                grouped[g, k] = work.tile([P, BANK, PACK], BF16, name="grouped%d" % k, align_bytes=64)
            return grouped[g, k][:, lo:hi, :], wl_raw[g, k][:, :, lo:hi]

        def interleave(copy, g, k, lo, hi):
            dst, src = interleave_views(g, k, lo, hi)
            copy(out=dst.rearrange("p (c i) t -> p c t i", i=4), in_=src.rearrange("p t (c i) -> p c t i", i=4))

        def interleave_gpsimd(g, k):
            dst, src = interleave_views(g, k, 0, BANK)
            nc.gpsimd.tensor_scalar(
                out=dst, in0=src.rearrange("p t n -> p n t"), scalar1=1.0, scalar2=1.0, op0=ALU.mult, op1=ALU.mult
            )

        def quantize_lever(g, k):
            wl_codes[g, k] = keep.tile([P, BANK], U32, name="wl_codes%d_%d" % (g, k), align_bytes=64)
            wl_plane[g, k] = keep.tile([P, BANK], U8, name="wl_plane%d_%d" % (g, k), align_bytes=64)
            nc.vector.quantize_mx(
                out=wl_codes[g, k][:].bitcast(FP8X4),
                scales=wl_plane[g, k][:],
                in_=grouped[g, k][:].rearrange("p n t -> p (n t)"),
            )

        def lever_product(s, passes=range(PASSES)):
            g, r = divmod(s, ROW_TILES)
            if s not in lever:
                lever[s] = next_product_bank()
            product(lever[s][:], r, lambda k: wl_codes[g, k][:].bitcast(FP8X4), lambda k: wl_plane[g, k][:], passes)

        def gravity_product(s):
            g, r = divmod(s, ROW_TILES)
            words, plane, at = (wg_first, wg_plane_first, 0) if g == 0 else (wg_rest, wg_plane_rest, BANK * (g - 1))
            gravity[s] = next_product_bank()
            product(
                gravity[s][:],
                r,
                lambda k: words[:, k, 2 * at : 2 * (at + BANK)].bitcast(FP4X4),
                lambda k: plane[:, k, at : at + BANK],
            )

        def scale_lever(s):
            scaled[s] = work.tile([P, P, J], F32, name="scaled", bufs=3)
            nc.vector.tensor_tensor(
                out=scaled[s][:],
                in0=lever[s][:].rearrange("p (c j) -> p c j", j=J),
                in1=load[s // BATCH][:, s % BATCH, :].unsqueeze(2).to_broadcast([P, P, J]),
                op=ALU.mult,
            )

        def add_gravity(s):
            g, r = divmod(s, ROW_TILES)
            torque[s] = work.tile([P, BANK], F32, name="torque", bufs=12)
            nc.vector.tensor_tensor(
                out=torque[s][:], in0=gravity[s][:], in1=scaled[s][:].rearrange("p c j -> p (c j)"), op=ALU.add
            )
            nc.sync.dma_start(out=out_0[r * P : (r + 1) * P, g * BANK : (g + 1) * BANK], in_=torque[s][:])

        def round_torque(s, copy):
            rounded[s] = work.tile([P, BANK], BF16, name="rounded", bufs=2 * BATCH)
            copy(
                out=rounded[s][:].rearrange("p (u m e) -> p u m e", u=2, e=2),
                in_=torque[s][:].rearrange("p (m u e) -> p u m e", u=2, e=2),
            )

        def turn(first, size):
            pair_words[first] = work.tile([P, size * P, 2], F32, name="pair_words", bufs=3, align_bytes=64)
            banks = []
            for lo in range(0, size, 2):
                banks.append(next_side_bank([P, 2, 2, P]))
                for a in range(2):
                    pairs = rounded[first + lo + a][:].bitcast(F32)
                    for u in range(2):
                        nc.tensor.transpose(banks[-1][:, a, u, :], pairs[:, u * P : (u + 1) * P], ident[:])
            return banks

        def empty_turned(first, banks):
            for n, bank in enumerate(banks):
                nc.scalar.copy(
                    out=pair_words[first][:, 2 * n * P : 2 * (n + 1) * P, :].rearrange("p (a m) u -> p a m u", a=2),
                    in_=bank[:].rearrange("p a u m -> p a m u"),
                )

        y_planes = keep.tile([P, T], U8, name="y_planes", align_bytes=64)
        out_words = out_1.rearrange("g p m t -> g p (m t)")

        def quantize_torque(first, size):
            g, r = divmod(first, ROW_TILES)
            codes = work.tile([P, size * P], U32, name="y_codes", bufs=4, align_bytes=64)
            nc.vector.quantize_mx(
                out=codes[:].bitcast(FP8X4),
                scales=y_planes[4 * g : P, r * P : (r + size) * P],
                in_=pair_words[first][:].rearrange("p m u -> p (m u)").bitcast(BF16),
            )
            nc.sync.dma_start(
                out=out_words[g][:, PACK * r * P : PACK * (r + size) * P].bitcast(I32), in_=codes[:].bitcast(I32)
            )

        bias_col = keep.tile([P, PACK], F32, name="bias_col")
        nc.scalar.copy(out=bias_col[:], in_=bias_raw[:])
        spread = next_side_bank([P, PACK, P])
        for i in range(PACK):
            nc.tensor.transpose(spread[:, i, :], bias_col[:, i : i + 1].to_broadcast([P, P]), ident[:])
        bias_row = keep.tile([P, P, PACK], F32, name="bias_row")

        interleave(nc.scalar.copy, 0, 0, VECTOR_COLUMNS, BANK)
        interleave(nc.vector.tensor_copy, 0, 0, 0, VECTOR_COLUMNS)
        nc.scalar.copy(out=bias_row[:], in_=spread[:].rearrange("p i m -> p m i"))
        quantize_lever(0, 0)
        lever_product(0, [0])
        lever_product(1, [0])
        force_product(0)
        interleave(nc.scalar.copy, 0, 1, VECTOR_COLUMNS, BANK)
        interleave(nc.vector.tensor_copy, 0, 1, 0, VECTOR_COLUMNS)
        quantize_lever(0, 1)
        interleave_gpsimd(1, 1)
        add_bias(0)
        sigmoid(0)
        lever_product(0, [1])
        gravity_product(0)
        lever_product(1, [1])

        force_at = {max(BATCH * b - FORCE_LEAD, 0): b for b in range(1, STEPS // BATCH)}
        piece_at = {}
        for g in range(1, GROUPS):
            for piece in range(PIECES):
                piece_at.setdefault(max((g - 1) * ROW_TILES - PIECE_LEAD + piece, 0), []).append((g, piece))
        width = BANK // PIECES

        for s in range(STEPS):
            g, r = divmod(s, ROW_TILES)
            scale_lever(s)
            if s - 1 in force_at:
                add_bias(force_at[s - 1])
            if g + 1 < GROUPS and r == QUANTIZE_AT[0]:
                quantize_lever(g + 1, 0)
            if s >= 1:
                add_gravity(s - 1)
                round_torque(s - 1, nc.scalar.copy)
            if s - 2 in force_at:
                sigmoid(force_at[s - 2])
            to_quantize = s - PLANES_LAG - (BATCH - 1)
            if to_quantize >= 0 and to_quantize % BATCH == 0:
                quantize_torque(to_quantize, BATCH)
            if g + 1 < GROUPS and r == QUANTIZE_AT[1]:
                quantize_lever(g + 1, 1)
                if g + 2 < GROUPS:
                    interleave_gpsimd(g + 2, 1)
            for next_group, piece in piece_at.get(s, []):
                interleave(nc.scalar.copy, next_group, 0, piece * width, (piece + 1) * width)
            if s + 1 < STEPS:
                gravity_product(s + 1)
            if s in force_at:
                force_product(force_at[s])
            if s + 2 < STEPS:
                lever_product(s + 2)
            to_turn = s - TURN_LAG - (BATCH - 1)
            if to_turn >= 0 and to_turn % BATCH == 0:
                empty_turned(to_turn, turn(to_turn, BATCH))

        last = STEPS - BATCH
        empty_turned(last, turn(last, 2))
        add_gravity(STEPS - 1)
        round_torque(STEPS - 1, nc.vector.tensor_copy)
        quantize_torque(last - BATCH, BATCH)
        final_banks = turn(last + 2, 2)
        quantize_torque(last, 2)
        empty_turned(last + 2, final_banks)
        quantize_torque(last + 2, 2)
        for q in range(QUADRANTS):
            queue = (nc.sync, nc.scalar)[q % 2]
            queue.dma_start(
                out=out_2[:, 4 * q : 4 * q + 4, :].bitcast(I32), in_=y_planes[32 * q : 32 * q + 16, :].bitcast(I32)
            )
